import numpy as np
import ml_dtypes


def mxq(x, axis, fmt="e4m3"):
    dtype, down = {"e4m3": (ml_dtypes.float8_e4m3fn, 7), "e5m2": (ml_dtypes.float8_e5m2, 14)}[fmt]
    v = np.moveaxis(np.asarray(x, np.float32).astype(ml_dtypes.bfloat16).astype(np.float64), axis, -1)
    blocks = v.reshape(v.shape[:-1] + (-1, 32))
    amax = np.abs(blocks).max(-1, keepdims=True)
    byte = np.maximum(np.where(amax > 0, np.frexp(amax)[1] - 1 + 127, 0) - down, 1)
    scale = np.exp2(byte - 127.0)
    codes = (blocks / scale).astype(np.float32).astype(dtype).astype(np.float64)
    return np.moveaxis((codes * scale).reshape(v.shape), -1, axis)


WIDE = False


def mx_kscale(k):
    if not WIDE:
        return np.ones(k)
    levels = np.array([10, -10, 5, -5, 0])
    if k % 512:
        return np.exp2(np.random.permutation(np.resize(levels, k // 32))).repeat(32)
    a = np.empty((k // 512, 16))
    for p in range(k // 512):
        a[p, :8] = np.random.permutation(np.resize(levels, 8))
        for g in range(8):
            far = levels[np.abs(levels - a[p, g]) >= 10]
            a[p, g + 8] = far[np.random.randint(len(far))]
    return np.exp2(a.ravel()).repeat(32)


def f64(x):
    return np.asarray(x).astype(np.float64)


def striped(idx):
    return np.tile(idx.reshape(-1, 16).T, (8, 1)).astype(np.uint16)


def unstriped(offs):
    return offs[:16].T.reshape(-1).astype(np.int64)


def striped8(idx):
    return np.concatenate([x.reshape(-1, 16).T for x in idx]).astype(np.uint16)


def runs(offs, k):
    lists = np.stack([offs[16 * r : 16 * r + 16].T.reshape(-1) for r in range(8)]).astype(np.int64)
    return lists[np.arange(k) % 512 // 64]


def pack_weight(w):
    k, n = w.shape
    w = f64(np.asarray(w, np.float32).astype(ml_dtypes.bfloat16)).reshape(k // 32, 32, n)
    amax = np.abs(w).max(1)
    byte = np.clip(np.where(amax > 0, np.frexp(amax)[1] - 1 + 127 - 7, 1), 1, 254)
    scaled = (w * np.exp2(127.0 - byte)[:, None, :]).reshape(k, n).astype(np.float32)
    words = np.ascontiguousarray(scaled.reshape(k // 512, 128, 4, n).transpose(0, 1, 3, 2)).astype(ml_dtypes.float8_e4m3fn).view(np.uint8)
    return words, np.ascontiguousarray(byte.astype(np.uint8).reshape(k // 512, 16, n))


def unpack_weight(words, scales):
    g, p, n, _ = words.shape
    vals = np.ascontiguousarray(words).view(ml_dtypes.float8_e4m3fn).astype(np.float64) * np.repeat(np.exp2(scales.astype(np.float64) - 127.0), 8, axis=1)[..., None]
    return vals.transpose(0, 1, 3, 2).reshape(g * 512, n)


def sigmoid(v):
    return 1.0 / (1.0 + np.exp(-np.maximum(v, -700.0)))

def planes(y):
    n, m = y.shape
    v = y.astype(np.float32).astype(ml_dtypes.bfloat16).astype(np.float64).reshape(n // 32, 32, m)
    top = np.abs(v).max(1)
    byte = np.clip(np.where(top > 0, np.frexp(top)[1] - 1 + 127 - 7, 1), 1, 254)
    codes = (v * np.exp2(127.0 - byte)[:, None, :]).reshape(n, m).astype(np.float32).astype(ml_dtypes.float8_e4m3fn).view(np.uint8)
    words = codes.reshape(n // 512, 128, 4, m).transpose(0, 1, 3, 2)
    return np.ascontiguousarray(words), np.ascontiguousarray(byte.astype(np.uint8).reshape(n // 512, 16, m))


K, T, S, N, H, G = 512, 2048, 256, 512, 512, 2048


def setup_inputs():
    n = np.random.standard_normal
    s = mx_kscale(K)[:, None]
    u = mx_kscale(K)
    packed_xT = pack_weight(n((K, T)) * s)
    packed_w1 = pack_weight(n((K, H)) / np.sqrt(K) / s)
    packed_w2 = pack_weight(n((H, N)) / np.sqrt(H) / u[:, None])
    packed_dT = pack_weight(n((K, G)) / s)
    return {
        "x_words": packed_xT[0],
        "x_scales": packed_xT[1],
        "w1_words": packed_w1[0],
        "w1_scales": packed_w1[1],
        "gn": (np.random.uniform(0.5, 1.5, (H, 1)) * u[:, None]).astype(np.float32),
        "w2_words": packed_w2[0],
        "w2_scales": packed_w2[1],
        "d_words": packed_dT[0],
        "d_scales": packed_dT[1],
        "offs": striped(np.random.permutation(T)[:S]),
        "n1": striped8(np.stack([np.random.permutation(S) for _ in range(8)])),
        "n2": striped8(np.stack([np.random.permutation(S) for _ in range(8)])),
        "two": striped(np.random.permutation(T)[:S]),
        "k1": striped8(np.random.randint(0, G, (8, H))),
        "n3": striped(np.random.permutation(S)),
        "n4": striped(np.random.permutation(S)),
    }


def reference(x_words, x_scales, w1_words, w1_scales, gn, w2_words, w2_scales, d_words, d_scales, offs, n1, n2, two, k1, n3, n4):
    xq = unpack_weight(x_words, x_scales)[:, unstriped(offs)]
    y = unpack_weight(w1_words, w1_scales).T @ xq
    st = y + y[np.arange(H)[:, None], runs(n1, H)]
    z = f64(gn) * (st * (np.tanh(st[np.arange(H)[:, None], runs(n2, H)])))
    a = unpack_weight(w2_words, w2_scales).T @ mxq(z, 0, "e4m3")
    d_k1 = unpack_weight(d_words, d_scales)[np.arange(K)[:, None], runs(k1, K)]
    x_two = unpack_weight(x_words, x_scales)[:, unstriped(two)]
    b = 0.0625 * (d_k1.T @ x_two)
    out_0 = a * (sigmoid(b[:, unstriped(n4)])) - (0.5 * a[:, unstriped(n3)])
    return (out_0,) + planes(out_0)

@@ -1,0 +1,212 @@
+from contextlib import ExitStack
+
+import concourse.mybir as mybir
+
+F32 = mybir.dt.float32
+BF16 = mybir.dt.bfloat16
+I32 = mybir.dt.int32
+U32 = mybir.dt.uint32
+U16 = mybir.dt.uint16
+U8 = mybir.dt.uint8
+FP8X4 = mybir.dt.float8_e4m3fn_x4
+ACT = mybir.ActivationFunctionType
+ALU = mybir.AluOpType
+
+P = 128
+PACK = 4
+K, T, S, N, H, G = 512, 2048, 256, 512, 512, 2048
+HALF = S // 2
+FLOPS = 3 * 2 * 512 * 512 * 256
+
+
+def words_of(dram):
+    return dram[0].rearrange("p n t -> p (n t)").bitcast(I32)
+
+
+def load_scale_rows(queue, tile, dram, quadrants):
+    for q in quadrants:
+        queue.dma_start(out=tile[32 * q : 32 * q + 4, :].bitcast(I32), in_=dram[0, 4 * q : 4 * q + 4, :].bitcast(I32))
+
+
+def dealt(tile):
+    return tile[:].rearrange("p (t m) -> p m t", t=PACK)
+
+
+def plain(tile):
+    return tile[:].rearrange("p (m t) -> p m t", t=PACK)
+
+
+def by_plane(tile):
+    return tile[:].rearrange("p (t m) -> p t m", t=PACK)
+
+
+def stepped(tile):
+    return tile[:].rearrange("p (m t) -> p t m", t=PACK)
+
+
+def half_list(offsets, h):
+    return offsets[:, h * HALF // 16 : (h + 1) * HALF // 16]
+
+
+def tile_picked_cdjoingatebhopp_none_po_kernel(
+    tc, x_words, x_scales, w1_words, w1_scales, gn, w2_words, w2_scales, d_words, d_scales,
+    offs, n1, n2, two, k1, n3, n4, out_0, out_1, out_2,
+):
+    nc = tc.nc
+    with ExitStack() as ctx:
+        keep = ctx.enter_context(tc.tile_pool(name="keep", bufs=1))
+        psum = ctx.enter_context(tc.psum_pool(name="psum", bufs=1))
+
+        def sb(name, shape, dtype):
+            return keep.tile(shape, dtype, name=name, align_bytes=64)
+
+        offs_l = sb("offs_l", [P, S // 16], U16)
+        two_l = sb("two_l", [P, S // 16], U16)
+        k1_l = sb("k1_l", [P, H // 16], U16)
+        n1_l = sb("n1_l", [P, S // 16], U16)
+        n2_l = sb("n2_l", [P, S // 16], U16)
+        n3_l = sb("n3_l", [P, S // 16], U16)
+        n4_l = sb("n4_l", [P, S // 16], U16)
+
+        x_w = sb("x_w", [P, T], U32)
+        x_s = sb("x_s", [P, T], U8)
+        d_w = sb("d_w", [P, G], U32)
+        d_s = sb("d_s", [P, G], U8)
+        w1_w = sb("w1_w", [P, H], U32)
+        w1_s = sb("w1_s", [P, H], U8)
+        w2_w = sb("w2_w", [P, N], U32)
+        w2_s = sb("w2_s", [P, N], U8)
+        gain = sb("gain", [P, PACK], F32)
+
+        nc.gpsimd.memset(d_s[:].bitcast(I32), 0)
+        nc.vector.memset(w1_s[:].bitcast(I32), 0)
+        nc.vector.memset(x_s[:].bitcast(I32), 0)
+        nc.vector.memset(w2_s[:].bitcast(I32), 0)
+        y = [sb(f"y{t}", [P, 2 * S], F32) for t in range(PACK)]
+        tb = sb("tb", [P, (PACK + 1) * S], F32)
+        for t in range(PACK):
+            nc.vector.memset(y[t][:, S:], 0.0)
+        nc.vector.memset(tb[:, PACK * S :], 0.0)
+
+        nc.sync.dma_start(k1_l[:], k1)
+        nc.scalar.dma_start(out=w1_w[:].bitcast(I32), in_=words_of(w1_words))
+        nc.sync.dma_start(offs_l[:], offs)
+        for e in range(2):
+            nc.scalar.dma_start(out=d_s[e:P:16, :].bitcast(I32), in_=d_scales[0, e:16:2, :].bitcast(I32))
+        nc.sync.dma_start(two_l[:], two)
+        nc.sync.dma_start(out=x_w[:].bitcast(I32), in_=words_of(x_words))
+        load_scale_rows(nc.scalar, w1_s, w1_scales, range(3))
+        load_scale_rows(nc.gpsimd, w1_s, w1_scales, range(3, 4))
+        load_scale_rows(nc.sync, x_s, x_scales, range(3))
+        load_scale_rows(nc.gpsimd, x_s, x_scales, range(3, 4))
+        nc.sync.dma_start(n1_l[:], n1)
+        nc.sync.dma_start(out=d_w[:].bitcast(I32), in_=words_of(d_words))
+
+        dq_s = sb("dq_s", [P, H], U8)
+        dq_w = sb("dq_w", [P, H], U32)
+        dd_s = sb("dd_s", [P, H], U8)
+        dp_s = sb("dp_s", [P, H], U8)
+        dd_w = sb("dd_w", [P, H], U32)
+        x2_s = sb("x2_s", [P, S], U8)
+        x2_w = sb("x2_w", [P, S], U32)
+        w1d_w = sb("w1d_w", [P, H], U32)
+        w1d_s = sb("w1d_s", [P, H], U8)
+        nc.vector.tensor_copy(dealt(w1d_w), plain(w1_w))
+        nc.vector.tensor_copy(dq_s[:], d_s[:].indirect(k1_l[:]))
+        nc.vector.tensor_copy(by_plane(dd_s), stepped(dq_s))
+        nc.vector.tensor_copy(dp_s[:].bitcast(I32), dd_s[:].bitcast(I32))
+        for e in range(2):
+            nc.sync.dma_start(out=dp_s[2 + e : P : 32, :].bitcast(I32), in_=dd_s[16 + e : P : 32, :].bitcast(I32))
+
+        nc.sync.dma_start(n2_l[:], n2)
+        nc.sync.dma_start(out=gain[:], in_=gn.rearrange("(p t) o -> p (t o)", t=PACK))
+        nc.sync.dma_start(out=w2_w[:].bitcast(I32), in_=words_of(w2_words))
+        load_scale_rows(nc.sync, w2_s, w2_scales, range(4))
+        nc.sync.dma_start(n4_l[:], n4)
+        nc.sync.dma_start(n3_l[:], n3)
+
+        xq_s = sb("xq_s", [P, S], U8)
+        xq_w = sb("xq_w", [P, S], U32)
+        nc.gpsimd.tensor_copy(by_plane(w1d_s), stepped(w1_s))
+        nc.vector.tensor_copy(xq_w[:], x_w[:].indirect(offs_l[:]))
+        nc.vector.tensor_copy(xq_s[:], x_s[:].indirect(offs_l[:]))
+        nc.vector.tensor_copy(x2_s[:], x_s[:].indirect(two_l[:]))
+
+        def product(bank, w, w_s, t, r, r_s):
+            cols = slice(t * P, (t + 1) * P)
+            nc.tensor.matmul_mx(
+                out=bank, lhsT=w[:, cols].bitcast(FP8X4), lhsT_scale=w_s[:, cols],
+                rhs=r.bitcast(FP8X4), rhs_scale=r_s, start=True, stop=True,
+            )
+
+        y_ps = [psum.tile([P, S], F32, name=f"y_ps{t}") for t in range(PACK)]
+        for t in range(PACK):
+            product(y_ps[t][:], w1d_w, w1d_s, t, xq_w[:], xq_s[:])
+        for t in range(PACK):
+            nc.vector.tensor_copy(y[t][:, :S], y_ps[t][:])
+        nc.vector.tensor_copy(x2_w[:], x_w[:].indirect(two_l[:]))
+
+        y_n1 = [sb(f"y_n1_{t}", [P, S], F32) for t in range(PACK)]
+        st = [sb(f"st{t}", [P, S], F32) for t in range(PACK)]
+        th = [sb(f"th{t}", [P, S], F32) for t in range(PACK)]
+        for t in range(PACK):
+            nc.scalar.activation(y_n1[t][:], y[t][:].indirect(n1_l[:]), ACT.Copy)
+            nc.vector.tensor_tensor(st[t][:], y_ps[t][:], y_n1[t][:], ALU.add)
+        for t in range(PACK):
+            nc.scalar.activation(th[t][:], st[t][:], ACT.Tanh)
+
+        nc.vector.tensor_copy(dq_w[:], d_w[:].indirect(k1_l[:]))
+        nc.vector.tensor_copy(dealt(dd_w), plain(dq_w))
+
+        b_ps = [psum.tile([P, 2, S], F32, name=f"b_ps{u}") for u in range(2)]
+        for t in range(PACK):
+            product(b_ps[t // 2][:, t % 2, :], dd_w, dp_s, t, x2_w[:], x2_s[:])
+
+        w2d_w = sb("w2d_w", [P, N], U32)
+        w2d_s = sb("w2d_s", [P, N], U8)
+        nc.gpsimd.tensor_copy(by_plane(w2d_w), stepped(w2_w))
+        nc.gpsimd.tensor_copy(by_plane(w2d_s), stepped(w2_s))
+
+        a_ps = [psum.tile([P, PACK, HALF], F32, name=f"a_ps{h}") for h in range(2)]
+        a = sb("a", [P, PACK, S], F32)
+        for h in range(2):
+            cols = slice(h * HALF, (h + 1) * HALF)
+            th_n2 = sb(f"th_n2_{h}", [P, PACK, HALF], F32)
+            z = sb(f"z{h}", [P, PACK, HALF], F32)
+            z_bf = sb(f"z_bf{h}", [P, HALF, PACK], BF16)
+            z_w = sb(f"z_w{h}", [P, HALF], U32)
+            z_s = sb(f"z_s{h}", [P, HALF], U8)
+            for t in range(PACK):
+                nc.scalar.activation(th_n2[:, t, :], th[t][:].indirect(half_list(n2_l, h)), ACT.Copy)
+                nc.vector.scalar_tensor_tensor(z[:, t, :], st[t][:, cols], gain[:, t : t + 1], th_n2[:, t, :], ALU.mult, ALU.mult)
+            nc.vector.tensor_copy(z_bf[:].rearrange("p (c i) t -> p c t i", i=4), z[:].rearrange("p t (c i) -> p c t i", i=4))
+            nc.vector.quantize_mx(out=z_w[:].bitcast(FP8X4), scales=z_s[:], in_=z_bf[:].rearrange("p c t -> p (c t)"))
+            for t in range(PACK):
+                product(a_ps[h][:, t, :], w2d_w, w2d_s, t, z_w[:], z_s[:])
+            nc.vector.tensor_scalar(a[:, :, cols], a_ps[h][:], -0.5, None, ALU.mult)
+
+        out_w = sb("out_w", [P, S], U32)
+        out_s = sb("out_s", [P, S], U8)
+        out_rows = out_0.rearrange("(p t) j -> p t j", t=PACK)
+        sg = sb("sg", [P, PACK, S], F32)
+        for u in range(2):
+            nc.scalar.activation(tb[:, 2 * u * S : (2 * u + 2) * S], b_ps[u][:].rearrange("p t j -> p (t j)"), ACT.Tanh, scale=0.03125)
+        for t in range(PACK):
+            nc.scalar.activation(sg[:, t, :], tb[:, t * S : (t + 2) * S].indirect(n4_l[:]), ACT.Copy)
+        for h in range(2):
+            cols = slice(h * HALF, (h + 1) * HALF)
+            a_n3 = sb(f"a_n3_{h}", [P, PACK, HALF], F32)
+            gated = sb(f"gated{h}", [P, PACK, HALF], F32)
+            res = sb(f"res{h}", [P, PACK, HALF], F32)
+            res_bf = sb(f"res_bf{h}", [P, HALF, PACK], BF16)
+            nc.vector.scalar_tensor_tensor(gated[:], sg[:, :, cols], 1.0, a_ps[h][:], ALU.add, ALU.mult)
+            for t in range(PACK):
+                nc.scalar.activation(a_n3[:, t, :], a[:, t, :].indirect(half_list(n3_l, h)), ACT.Copy)
+            nc.vector.scalar_tensor_tensor(res[:], gated[:], 0.5, a_n3[:], ALU.mult, ALU.add)
+            nc.sync.dma_start(out=out_rows[:, :, cols], in_=res[:])
+            nc.vector.tensor_copy(res_bf[:].rearrange("p (c i) t -> p c t i", i=4), res[:].rearrange("p t (c i) -> p c t i", i=4))
+            nc.vector.quantize_mx(out=out_w[:, cols].bitcast(FP8X4), scales=out_s[:, cols], in_=res_bf[:].rearrange("p c t -> p (c t)"))
+            nc.sync.dma_start(out=words_of(out_1)[:, cols], in_=out_w[:, cols].bitcast(I32))
+        for q in range(4):
+            queue = nc.sync if q % 2 == 0 else nc.scalar
+            queue.dma_start(out=out_2[0, 4 * q : 4 * q + 4, :].bitcast(I32), in_=out_s[32 * q : 32 * q + 4, :].bitcast(I32))

@@ -16,6 +16,7 @@ P = 128
 PACK = 4
 K, T, S, N, H, G = 512, 2048, 256, 512, 512, 2048
 HALF = S // 2
+BIG = 2.0**126
 FLOPS = 3 * 2 * 512 * 512 * 256
 
 
@@ -78,32 +79,30 @@ def tile_picked_cdjoingatebhopp_none_po_kernel(
         w2_s = sb("w2_s", [P, N], U8)
         gain = sb("gain", [P, PACK], F32)
 
-        nc.gpsimd.memset(d_s[:].bitcast(I32), 0)
+        nc.vector.memset(d_s[:, : G // 2].bitcast(I32), 0)
+        nc.gpsimd.memset(d_s[:, G // 2 :].bitcast(I32), 0)
         nc.vector.memset(w1_s[:].bitcast(I32), 0)
-        nc.vector.memset(x_s[:].bitcast(I32), 0)
-        nc.vector.memset(w2_s[:].bitcast(I32), 0)
+        nc.vector.memset(x_s[:, : T // 2].bitcast(I32), 0)
+        nc.gpsimd.memset(x_s[:, T // 2 :].bitcast(I32), 0)
         y = [sb(f"y{t}", [P, 2 * S], F32) for t in range(PACK)]
-        tb = sb("tb", [P, (PACK + 1) * S], F32)
-        for t in range(PACK):
-            nc.vector.memset(y[t][:, S:], 0.0)
-        nc.vector.memset(tb[:, PACK * S :], 0.0)
+        for window in y:
+            nc.gpsimd.memset(window[:, S:], 0.0)
+        nc.gpsimd.memset(w2_s[:].bitcast(I32), 0)
 
         nc.sync.dma_start(k1_l[:], k1)
-        nc.scalar.dma_start(out=w1_w[:].bitcast(I32), in_=words_of(w1_words))
         nc.sync.dma_start(offs_l[:], offs)
+        nc.sync.dma_start(n1_l[:], n1)
+        nc.sync.dma_start(out=gain[:], in_=gn.rearrange("(p t) o -> p (t o)", t=PACK))
+        nc.sync.dma_start(out=w1_w[:].bitcast(I32), in_=words_of(w1_words))
         for e in range(2):
-            nc.scalar.dma_start(out=d_s[e:P:16, :].bitcast(I32), in_=d_scales[0, e:16:2, :].bitcast(I32))
-        nc.sync.dma_start(two_l[:], two)
+            nc.sync.dma_start(out=d_s[e:P:16, :].bitcast(I32), in_=d_scales[0, e:16:2, :].bitcast(I32))
         nc.sync.dma_start(out=x_w[:].bitcast(I32), in_=words_of(x_words))
-        load_scale_rows(nc.scalar, w1_s, w1_scales, range(3))
-        load_scale_rows(nc.gpsimd, w1_s, w1_scales, range(3, 4))
+        load_scale_rows(nc.sync, w1_s, w1_scales, range(4))
         load_scale_rows(nc.sync, x_s, x_scales, range(3))
         load_scale_rows(nc.gpsimd, x_s, x_scales, range(3, 4))
-        nc.sync.dma_start(n1_l[:], n1)
-        nc.sync.dma_start(out=d_w[:].bitcast(I32), in_=words_of(d_words))
 
         dq_s = sb("dq_s", [P, H], U8)
-        dq_w = sb("dq_w", [P, H], U32)
+        dq_w = keep.tile([P, H], U32, name="dq_w", tag="dq_w", align_bytes=64)
         dd_s = sb("dd_s", [P, H], U8)
         dp_s = sb("dp_s", [P, H], U8)
         dd_w = sb("dd_w", [P, H], U32)
@@ -111,26 +110,30 @@ def tile_picked_cdjoingatebhopp_none_po_kernel(
         x2_w = sb("x2_w", [P, S], U32)
         w1d_w = sb("w1d_w", [P, H], U32)
         w1d_s = sb("w1d_s", [P, H], U8)
+        ungain = sb("ungain", [P, PACK], F32)
+        ungain_raw = sb("ungain_raw", [P, PACK], F32)
+        nc.vector.reciprocal(ungain_raw[:], gain[:])
         nc.vector.tensor_copy(dealt(w1d_w), plain(w1_w))
+        nc.vector.tensor_scalar(ungain[:], ungain_raw[:], BIG, -BIG, ALU.min, ALU.max)
         nc.vector.tensor_copy(dq_s[:], d_s[:].indirect(k1_l[:]))
         nc.vector.tensor_copy(by_plane(dd_s), stepped(dq_s))
         nc.vector.tensor_copy(dp_s[:].bitcast(I32), dd_s[:].bitcast(I32))
         for e in range(2):
             nc.sync.dma_start(out=dp_s[2 + e : P : 32, :].bitcast(I32), in_=dd_s[16 + e : P : 32, :].bitcast(I32))
 
+        nc.sync.dma_start(two_l[:], two)
         nc.sync.dma_start(n2_l[:], n2)
-        nc.sync.dma_start(out=gain[:], in_=gn.rearrange("(p t) o -> p (t o)", t=PACK))
+        nc.sync.dma_start(out=d_w[:].bitcast(I32), in_=words_of(d_words))
         nc.sync.dma_start(out=w2_w[:].bitcast(I32), in_=words_of(w2_words))
-        load_scale_rows(nc.sync, w2_s, w2_scales, range(4))
+        load_scale_rows(nc.gpsimd, w2_s, w2_scales, range(4))
         nc.sync.dma_start(n4_l[:], n4)
         nc.sync.dma_start(n3_l[:], n3)
 
         xq_s = sb("xq_s", [P, S], U8)
         xq_w = sb("xq_w", [P, S], U32)
-        nc.gpsimd.tensor_copy(by_plane(w1d_s), stepped(w1_s))
         nc.vector.tensor_copy(xq_w[:], x_w[:].indirect(offs_l[:]))
+        nc.vector.tensor_copy(by_plane(w1d_s), stepped(w1_s))
         nc.vector.tensor_copy(xq_s[:], x_s[:].indirect(offs_l[:]))
-        nc.vector.tensor_copy(x2_s[:], x_s[:].indirect(two_l[:]))
 
         def product(bank, w, w_s, t, r, r_s):
             cols = slice(t * P, (t + 1) * P)
@@ -142,18 +145,22 @@ def tile_picked_cdjoingatebhopp_none_po_kernel(
         y_ps = [psum.tile([P, S], F32, name=f"y_ps{t}") for t in range(PACK)]
         for t in range(PACK):
             product(y_ps[t][:], w1d_w, w1d_s, t, xq_w[:], xq_s[:])
-        for t in range(PACK):
-            nc.vector.tensor_copy(y[t][:, :S], y_ps[t][:])
-        nc.vector.tensor_copy(x2_w[:], x_w[:].indirect(two_l[:]))
+        nc.scalar.activation(y[0][:, :S], y_ps[0][:], ACT.Copy, scale=gain[:, 0:1])
+        for t in range(1, PACK):
+            nc.vector.tensor_scalar(y[t][:, :S], y_ps[t][:], gain[:, t : t + 1], None, ALU.mult)
 
         y_n1 = [sb(f"y_n1_{t}", [P, S], F32) for t in range(PACK)]
-        st = [sb(f"st{t}", [P, S], F32) for t in range(PACK)]
+        gst = sb("gst", [P, PACK, S], F32)
         th = [sb(f"th{t}", [P, S], F32) for t in range(PACK)]
         for t in range(PACK):
             nc.scalar.activation(y_n1[t][:], y[t][:].indirect(n1_l[:]), ACT.Copy)
-            nc.vector.tensor_tensor(st[t][:], y_ps[t][:], y_n1[t][:], ALU.add)
+            nc.vector.tensor_tensor(gst[:, t, :], y[t][:, :S], y_n1[t][:], ALU.add)
+            if t == 0:
+                nc.vector.tensor_copy(x2_s[:], x_s[:].indirect(two_l[:]))
+            if t == 1:
+                nc.vector.tensor_copy(x2_w[:], x_w[:].indirect(two_l[:]))
         for t in range(PACK):
-            nc.scalar.activation(th[t][:], st[t][:], ACT.Tanh)
+            nc.scalar.activation(th[t][:], gst[:, t, :], ACT.Tanh, scale=ungain[:, t : t + 1])
 
         nc.vector.tensor_copy(dq_w[:], d_w[:].indirect(k1_l[:]))
         nc.vector.tensor_copy(dealt(dd_w), plain(dq_w))
@@ -161,6 +168,7 @@ def tile_picked_cdjoingatebhopp_none_po_kernel(
         b_ps = [psum.tile([P, 2, S], F32, name=f"b_ps{u}") for u in range(2)]
         for t in range(PACK):
             product(b_ps[t // 2][:, t % 2, :], dd_w, dp_s, t, x2_w[:], x2_s[:])
+        b = y
 
         w2d_w = sb("w2d_w", [P, N], U32)
         w2d_s = sb("w2d_s", [P, N], U8)
@@ -169,44 +177,58 @@ def tile_picked_cdjoingatebhopp_none_po_kernel(
 
         a_ps = [psum.tile([P, PACK, HALF], F32, name=f"a_ps{h}") for h in range(2)]
         a = sb("a", [P, PACK, S], F32)
+        z_both = keep.tile([P, S * PACK], BF16, name="z_both", tag="dq_w", align_bytes=64)
         for h in range(2):
             cols = slice(h * HALF, (h + 1) * HALF)
             th_n2 = sb(f"th_n2_{h}", [P, PACK, HALF], F32)
-            z = sb(f"z{h}", [P, PACK, HALF], F32)
-            z_bf = sb(f"z_bf{h}", [P, HALF, PACK], BF16)
+            z_bf = z_both[:, h * HALF * PACK : (h + 1) * HALF * PACK]
             z_w = sb(f"z_w{h}", [P, HALF], U32)
             z_s = sb(f"z_s{h}", [P, HALF], U8)
             for t in range(PACK):
                 nc.scalar.activation(th_n2[:, t, :], th[t][:].indirect(half_list(n2_l, h)), ACT.Copy)
-                nc.vector.scalar_tensor_tensor(z[:, t, :], st[t][:, cols], gain[:, t : t + 1], th_n2[:, t, :], ALU.mult, ALU.mult)
-            nc.vector.tensor_copy(z_bf[:].rearrange("p (c i) t -> p c t i", i=4), z[:].rearrange("p t (c i) -> p c t i", i=4))
-            nc.vector.quantize_mx(out=z_w[:].bitcast(FP8X4), scales=z_s[:], in_=z_bf[:].rearrange("p c t -> p (c t)"))
+            nc.vector.tensor_tensor(
+                z_bf.rearrange("p (c i t) -> p c t i", i=4, t=PACK),
+                gst[:, :, cols].rearrange("p t (c i) -> p c t i", i=4),
+                th_n2[:].rearrange("p t (c i) -> p c t i", i=4),
+                ALU.mult,
+            )
+            nc.vector.quantize_mx(out=z_w[:].bitcast(FP8X4), scales=z_s[:], in_=z_bf)
             for t in range(PACK):
                 product(a_ps[h][:, t, :], w2d_w, w2d_s, t, z_w[:], z_s[:])
-            nc.vector.tensor_scalar(a[:, :, cols], a_ps[h][:], -0.5, None, ALU.mult)
+            for t in range(2 * h, 2 * h + 2):
+                nc.vector.tensor_copy(b[t][:, :S], b_ps[h][:, t % 2, :])
+        for h in range(2):
+            nc.vector.tensor_copy(a[:, :, h * HALF : (h + 1) * HALF], a_ps[h][:])
 
         out_w = sb("out_w", [P, S], U32)
         out_s = sb("out_s", [P, S], U8)
         out_rows = out_0.rearrange("(p t) j -> p t j", t=PACK)
         sg = sb("sg", [P, PACK, S], F32)
-        for u in range(2):
-            nc.scalar.activation(tb[:, 2 * u * S : (2 * u + 2) * S], b_ps[u][:].rearrange("p t j -> p (t j)"), ACT.Tanh, scale=0.03125)
         for t in range(PACK):
-            nc.scalar.activation(sg[:, t, :], tb[:, t * S : (t + 2) * S].indirect(n4_l[:]), ACT.Copy)
+            nc.scalar.activation(sg[:, t, :], b[t][:].indirect(n4_l[:]), ACT.Sigmoid, scale=0.0625)
+        a_n3 = [sb(f"a_n3_{h}", [P, PACK, HALF], F32) for h in range(2)]
+        gated = [sb(f"gated{h}", [P, PACK, HALF], F32) for h in range(2)]
+        res = [sb(f"res{h}", [P, PACK, HALF], F32) for h in range(2)]
+        res_bf = sb("res_bf", [P, S * PACK], BF16)
         for h in range(2):
             cols = slice(h * HALF, (h + 1) * HALF)
-            a_n3 = sb(f"a_n3_{h}", [P, PACK, HALF], F32)
-            gated = sb(f"gated{h}", [P, PACK, HALF], F32)
-            res = sb(f"res{h}", [P, PACK, HALF], F32)
-            res_bf = sb(f"res_bf{h}", [P, HALF, PACK], BF16)
-            nc.vector.scalar_tensor_tensor(gated[:], sg[:, :, cols], 1.0, a_ps[h][:], ALU.add, ALU.mult)
-            for t in range(PACK):
-                nc.scalar.activation(a_n3[:, t, :], a[:, t, :].indirect(half_list(n3_l, h)), ACT.Copy)
-            nc.vector.scalar_tensor_tensor(res[:], gated[:], 0.5, a_n3[:], ALU.mult, ALU.add)
-            nc.sync.dma_start(out=out_rows[:, :, cols], in_=res[:])
-            nc.vector.tensor_copy(res_bf[:].rearrange("p (c i) t -> p c t i", i=4), res[:].rearrange("p t (c i) -> p c t i", i=4))
-            nc.vector.quantize_mx(out=out_w[:, cols].bitcast(FP8X4), scales=out_s[:, cols], in_=res_bf[:].rearrange("p c t -> p (c t)"))
-            nc.sync.dma_start(out=words_of(out_1)[:, cols], in_=out_w[:, cols].bitcast(I32))
+            nc.vector.tensor_tensor(gated[h][:], a_ps[h][:], sg[:, :, cols], ALU.mult)
+            for t in range(PACK - 1):
+                nc.scalar.activation(a_n3[h][:, t, :], a[:, t, :].indirect(half_list(n3_l, h)), ACT.Copy)
+            nc.vector.tensor_copy(a_n3[h][:, PACK - 1, :], a[:, PACK - 1, :].indirect(half_list(n3_l, h)))
+        for h in range(2):
+            cols = slice(h * HALF, (h + 1) * HALF)
+            nc.vector.scalar_tensor_tensor(res[h][:], a_n3[h][:], -0.5, gated[h][:], ALU.mult, ALU.add)
+            nc.sync.dma_start(out=out_rows[:, :, cols], in_=res[h][:])
+        for h in range(2):
+            woven = res_bf[:, h * HALF * PACK : (h + 1) * HALF * PACK].rearrange("p (c i t) -> p c t i", i=4, t=PACK)
+            rows = res[h][:].rearrange("p t (c i) -> p c t i", i=4)
+            if h == 0:
+                nc.scalar.copy(woven, rows)
+            else:
+                nc.vector.tensor_copy(woven, rows)
+        nc.vector.quantize_mx(out=out_w[:].bitcast(FP8X4), scales=out_s[:], in_=res_bf[:])
+        nc.sync.dma_start(out=words_of(out_1), in_=out_w[:].bitcast(I32))
         for q in range(4):
-            queue = nc.sync if q % 2 == 0 else nc.scalar
+            queue = nc.sync if q == 0 else nc.scalar
             queue.dma_start(out=out_2[0, 4 * q : 4 * q + 4, :].bitcast(I32), in_=out_s[32 * q : 32 * q + 4, :].bitcast(I32))

@@ -91,15 +91,15 @@ def tile_picked_cdjoingatebhopp_none_po_kernel(
 
         nc.sync.dma_start(k1_l[:], k1)
         nc.sync.dma_start(offs_l[:], offs)
-        nc.sync.dma_start(n1_l[:], n1)
         nc.sync.dma_start(out=gain[:], in_=gn.rearrange("(p t) o -> p (t o)", t=PACK))
         nc.sync.dma_start(out=w1_w[:].bitcast(I32), in_=words_of(w1_words))
         for e in range(2):
             nc.sync.dma_start(out=d_s[e:P:16, :].bitcast(I32), in_=d_scales[0, e:16:2, :].bitcast(I32))
+        load_scale_rows(nc.sync, w1_s, w1_scales, range(1))
         nc.sync.dma_start(out=x_w[:].bitcast(I32), in_=words_of(x_words))
-        load_scale_rows(nc.sync, w1_s, w1_scales, range(4))
-        load_scale_rows(nc.sync, x_s, x_scales, range(3))
-        load_scale_rows(nc.gpsimd, x_s, x_scales, range(3, 4))
+        load_scale_rows(nc.sync, w1_s, w1_scales, range(1, 4))
+        load_scale_rows(nc.sync, x_s, x_scales, range(4))
+        nc.sync.dma_start(n1_l[:], n1)
 
         dq_s = sb("dq_s", [P, H], U8)
         dq_w = keep.tile([P, H], U32, name="dq_w", tag="dq_w", align_bytes=64)
@@ -125,7 +125,7 @@ def tile_picked_cdjoingatebhopp_none_po_kernel(
         nc.sync.dma_start(n2_l[:], n2)
         nc.sync.dma_start(out=d_w[:].bitcast(I32), in_=words_of(d_words))
         nc.sync.dma_start(out=w2_w[:].bitcast(I32), in_=words_of(w2_words))
-        load_scale_rows(nc.gpsimd, w2_s, w2_scales, range(4))
+        load_scale_rows(nc.sync, w2_s, w2_scales, range(4))
         nc.sync.dma_start(n4_l[:], n4)
         nc.sync.dma_start(n3_l[:], n3)
 
@@ -172,8 +172,8 @@ def tile_picked_cdjoingatebhopp_none_po_kernel(
 
         w2d_w = sb("w2d_w", [P, N], U32)
         w2d_s = sb("w2d_s", [P, N], U8)
-        nc.gpsimd.tensor_copy(by_plane(w2d_w), stepped(w2_w))
-        nc.gpsimd.tensor_copy(by_plane(w2d_s), stepped(w2_s))
+        nc.vector.tensor_copy(dealt(w2d_w), plain(w2_w))
+        nc.vector.tensor_copy(by_plane(w2d_s), stepped(w2_s))
 
         a_ps = [psum.tile([P, PACK, HALF], F32, name=f"a_ps{h}") for h in range(2)]
         a = sb("a", [P, PACK, S], F32)

from contextlib import ExitStack

import concourse.mybir as mybir

F32 = mybir.dt.float32
BF16 = mybir.dt.bfloat16
I32 = mybir.dt.int32
U32 = mybir.dt.uint32
U16 = mybir.dt.uint16
U8 = mybir.dt.uint8
FP8X4 = mybir.dt.float8_e4m3fn_x4
ACT = mybir.ActivationFunctionType
ALU = mybir.AluOpType

P = 128
PACK = 4
K, T, S, N, H, G = 512, 2048, 256, 512, 512, 2048
HALF = S // 2
BIG = 2.0**126
FLOPS = 3 * 2 * 512 * 512 * 256


def words_of(dram):
    return dram[0].rearrange("p n t -> p (n t)").bitcast(I32)


def load_scale_rows(queue, tile, dram, quadrants):
    for q in quadrants:
        queue.dma_start(out=tile[32 * q : 32 * q + 4, :].bitcast(I32), in_=dram[0, 4 * q : 4 * q + 4, :].bitcast(I32))


def dealt(tile):
    return tile[:].rearrange("p (t m) -> p m t", t=PACK)


def plain(tile):
    return tile[:].rearrange("p (m t) -> p m t", t=PACK)


def by_plane(tile):
    return tile[:].rearrange("p (t m) -> p t m", t=PACK)


def stepped(tile):
    return tile[:].rearrange("p (m t) -> p t m", t=PACK)


def half_list(offsets, h):
    return offsets[:, h * HALF // 16 : (h + 1) * HALF // 16]


def tile_picked_cdjoingatebhopp_none_po_kernel(
    tc, x_words, x_scales, w1_words, w1_scales, gn, w2_words, w2_scales, d_words, d_scales,
    offs, n1, n2, two, k1, n3, n4, out_0, out_1, out_2,
):
    nc = tc.nc
    with ExitStack() as ctx:
        keep = ctx.enter_context(tc.tile_pool(name="keep", bufs=1))
        psum = ctx.enter_context(tc.psum_pool(name="psum", bufs=1))

        def sb(name, shape, dtype):
            return keep.tile(shape, dtype, name=name, align_bytes=64)

        offs_l = sb("offs_l", [P, S // 16], U16)
        two_l = sb("two_l", [P, S // 16], U16)
        k1_l = sb("k1_l", [P, H // 16], U16)
        n1_l = sb("n1_l", [P, S // 16], U16)
        n2_l = sb("n2_l", [P, S // 16], U16)
        n3_l = sb("n3_l", [P, S // 16], U16)
        n4_l = sb("n4_l", [P, S // 16], U16)

        x_w = sb("x_w", [P, T], U32)
        x_s = sb("x_s", [P, T], U8)
        d_w = sb("d_w", [P, G], U32)
        d_s = sb("d_s", [P, G], U8)
        w1_w = sb("w1_w", [P, H], U32)
        w1_s = sb("w1_s", [P, H], U8)
        w2_w = sb("w2_w", [P, N], U32)
        w2_s = sb("w2_s", [P, N], U8)
        gain = sb("gain", [P, PACK], F32)

        nc.vector.memset(d_s[:, : G // 2].bitcast(I32), 0)
        nc.gpsimd.memset(d_s[:, G // 2 :].bitcast(I32), 0)
        nc.vector.memset(w1_s[:].bitcast(I32), 0)
        nc.vector.memset(x_s[:, : T // 2].bitcast(I32), 0)
        nc.gpsimd.memset(x_s[:, T // 2 :].bitcast(I32), 0)
        y = [sb(f"y{t}", [P, 2 * S], F32) for t in range(PACK)]
        for window in y:
            nc.gpsimd.memset(window[:, S:], 0.0)
        nc.gpsimd.memset(w2_s[:].bitcast(I32), 0)

        nc.sync.dma_start(k1_l[:], k1)
        nc.sync.dma_start(offs_l[:], offs)
        nc.sync.dma_start(out=gain[:], in_=gn.rearrange("(p t) o -> p (t o)", t=PACK))
        nc.sync.dma_start(out=w1_w[:].bitcast(I32), in_=words_of(w1_words))
        for e in range(2):
            nc.sync.dma_start(out=d_s[e:P:16, :].bitcast(I32), in_=d_scales[0, e:16:2, :].bitcast(I32))
        load_scale_rows(nc.sync, w1_s, w1_scales, range(1))
        nc.sync.dma_start(out=x_w[:].bitcast(I32), in_=words_of(x_words))
        load_scale_rows(nc.sync, w1_s, w1_scales, range(1, 4))
        load_scale_rows(nc.sync, x_s, x_scales, range(4))
        nc.sync.dma_start(n1_l[:], n1)

        dq_s = sb("dq_s", [P, H], U8)
        dq_w = keep.tile([P, H], U32, name="dq_w", tag="dq_w", align_bytes=64)
        dd_s = sb("dd_s", [P, H], U8)
        dp_s = sb("dp_s", [P, H], U8)
        dd_w = sb("dd_w", [P, H], U32)
        x2_s = sb("x2_s", [P, S], U8)
        x2_w = sb("x2_w", [P, S], U32)
        w1d_w = sb("w1d_w", [P, H], U32)
        w1d_s = sb("w1d_s", [P, H], U8)
        ungain = sb("ungain", [P, PACK], F32)
        ungain_raw = sb("ungain_raw", [P, PACK], F32)
        nc.vector.reciprocal(ungain_raw[:], gain[:])
        nc.vector.tensor_copy(dealt(w1d_w), plain(w1_w))
        nc.vector.tensor_scalar(ungain[:], ungain_raw[:], BIG, -BIG, ALU.min, ALU.max)
        nc.vector.tensor_copy(dq_s[:], d_s[:].indirect(k1_l[:]))
        nc.vector.tensor_copy(by_plane(dd_s), stepped(dq_s))
        nc.vector.tensor_copy(dp_s[:].bitcast(I32), dd_s[:].bitcast(I32))
        for e in range(2):
            nc.sync.dma_start(out=dp_s[2 + e : P : 32, :].bitcast(I32), in_=dd_s[16 + e : P : 32, :].bitcast(I32))

        nc.sync.dma_start(two_l[:], two)
        nc.sync.dma_start(n2_l[:], n2)
        nc.sync.dma_start(out=d_w[:].bitcast(I32), in_=words_of(d_words))
        nc.sync.dma_start(out=w2_w[:].bitcast(I32), in_=words_of(w2_words))
        load_scale_rows(nc.sync, w2_s, w2_scales, range(4))
        nc.sync.dma_start(n4_l[:], n4)
        nc.sync.dma_start(n3_l[:], n3)

        xq_s = sb("xq_s", [P, S], U8)
        xq_w = sb("xq_w", [P, S], U32)
        nc.vector.tensor_copy(xq_w[:], x_w[:].indirect(offs_l[:]))
        nc.vector.tensor_copy(by_plane(w1d_s), stepped(w1_s))
        nc.vector.tensor_copy(xq_s[:], x_s[:].indirect(offs_l[:]))

        def product(bank, w, w_s, t, r, r_s):
            cols = slice(t * P, (t + 1) * P)
            nc.tensor.matmul_mx(
                out=bank, lhsT=w[:, cols].bitcast(FP8X4), lhsT_scale=w_s[:, cols],
                rhs=r.bitcast(FP8X4), rhs_scale=r_s, start=True, stop=True,
            )

        y_ps = [psum.tile([P, S], F32, name=f"y_ps{t}") for t in range(PACK)]
        for t in range(PACK):
            product(y_ps[t][:], w1d_w, w1d_s, t, xq_w[:], xq_s[:])
        nc.scalar.activation(y[0][:, :S], y_ps[0][:], ACT.Copy, scale=gain[:, 0:1])
        for t in range(1, PACK):
            nc.vector.tensor_scalar(y[t][:, :S], y_ps[t][:], gain[:, t : t + 1], None, ALU.mult)

        y_n1 = [sb(f"y_n1_{t}", [P, S], F32) for t in range(PACK)]
        gst = sb("gst", [P, PACK, S], F32)
        th = [sb(f"th{t}", [P, S], F32) for t in range(PACK)]
        for t in range(PACK):
            nc.scalar.activation(y_n1[t][:], y[t][:].indirect(n1_l[:]), ACT.Copy)
            nc.vector.tensor_tensor(gst[:, t, :], y[t][:, :S], y_n1[t][:], ALU.add)
            if t == 0:
                nc.vector.tensor_copy(x2_s[:], x_s[:].indirect(two_l[:]))
            if t == 1:
                nc.vector.tensor_copy(x2_w[:], x_w[:].indirect(two_l[:]))
        for t in range(PACK):
            nc.scalar.activation(th[t][:], gst[:, t, :], ACT.Tanh, scale=ungain[:, t : t + 1])

        nc.vector.tensor_copy(dq_w[:], d_w[:].indirect(k1_l[:]))
        nc.vector.tensor_copy(dealt(dd_w), plain(dq_w))

        b_ps = [psum.tile([P, 2, S], F32, name=f"b_ps{u}") for u in range(2)]
        for t in range(PACK):
            product(b_ps[t // 2][:, t % 2, :], dd_w, dp_s, t, x2_w[:], x2_s[:])
        b = y

        w2d_w = sb("w2d_w", [P, N], U32)
        w2d_s = sb("w2d_s", [P, N], U8)
        nc.vector.tensor_copy(dealt(w2d_w), plain(w2_w))
        nc.vector.tensor_copy(by_plane(w2d_s), stepped(w2_s))

        a_ps = [psum.tile([P, PACK, HALF], F32, name=f"a_ps{h}") for h in range(2)]
        a = sb("a", [P, PACK, S], F32)
        z_both = keep.tile([P, S * PACK], BF16, name="z_both", tag="dq_w", align_bytes=64)
        for h in range(2):
            cols = slice(h * HALF, (h + 1) * HALF)
            th_n2 = sb(f"th_n2_{h}", [P, PACK, HALF], F32)
            z_bf = z_both[:, h * HALF * PACK : (h + 1) * HALF * PACK]
            z_w = sb(f"z_w{h}", [P, HALF], U32)
            z_s = sb(f"z_s{h}", [P, HALF], U8)
            for t in range(PACK):
                nc.scalar.activation(th_n2[:, t, :], th[t][:].indirect(half_list(n2_l, h)), ACT.Copy)
            nc.vector.tensor_tensor(
                z_bf.rearrange("p (c i t) -> p c t i", i=4, t=PACK),
                gst[:, :, cols].rearrange("p t (c i) -> p c t i", i=4),
                th_n2[:].rearrange("p t (c i) -> p c t i", i=4),
                ALU.mult,
            )
            nc.vector.quantize_mx(out=z_w[:].bitcast(FP8X4), scales=z_s[:], in_=z_bf)
            for t in range(PACK):
                product(a_ps[h][:, t, :], w2d_w, w2d_s, t, z_w[:], z_s[:])
            for t in range(2 * h, 2 * h + 2):
                nc.vector.tensor_copy(b[t][:, :S], b_ps[h][:, t % 2, :])
        for h in range(2):
            nc.vector.tensor_copy(a[:, :, h * HALF : (h + 1) * HALF], a_ps[h][:])

        out_w = sb("out_w", [P, S], U32)
        out_s = sb("out_s", [P, S], U8)
        out_rows = out_0.rearrange("(p t) j -> p t j", t=PACK)
        sg = sb("sg", [P, PACK, S], F32)
        for t in range(PACK):
            nc.scalar.activation(sg[:, t, :], b[t][:].indirect(n4_l[:]), ACT.Sigmoid, scale=0.0625)
        a_n3 = [sb(f"a_n3_{h}", [P, PACK, HALF], F32) for h in range(2)]
        gated = [sb(f"gated{h}", [P, PACK, HALF], F32) for h in range(2)]
        res = [sb(f"res{h}", [P, PACK, HALF], F32) for h in range(2)]
        res_bf = sb("res_bf", [P, S * PACK], BF16)
        for h in range(2):
            cols = slice(h * HALF, (h + 1) * HALF)
            nc.vector.tensor_tensor(gated[h][:], a_ps[h][:], sg[:, :, cols], ALU.mult)
            for t in range(PACK - 1):
                nc.scalar.activation(a_n3[h][:, t, :], a[:, t, :].indirect(half_list(n3_l, h)), ACT.Copy)
            nc.vector.tensor_copy(a_n3[h][:, PACK - 1, :], a[:, PACK - 1, :].indirect(half_list(n3_l, h)))
        for h in range(2):
            cols = slice(h * HALF, (h + 1) * HALF)
            nc.vector.scalar_tensor_tensor(res[h][:], a_n3[h][:], -0.5, gated[h][:], ALU.mult, ALU.add)
            nc.sync.dma_start(out=out_rows[:, :, cols], in_=res[h][:])
        for h in range(2):
            woven = res_bf[:, h * HALF * PACK : (h + 1) * HALF * PACK].rearrange("p (c i t) -> p c t i", i=4, t=PACK)
            rows = res[h][:].rearrange("p t (c i) -> p c t i", i=4)
            if h == 0:
                nc.scalar.copy(woven, rows)
            else:
                nc.vector.tensor_copy(woven, rows)
        nc.vector.quantize_mx(out=out_w[:].bitcast(FP8X4), scales=out_s[:], in_=res_bf[:])
        nc.sync.dma_start(out=words_of(out_1), in_=out_w[:].bitcast(I32))
        for q in range(4):
            queue = nc.sync if q == 0 else nc.scalar
            queue.dma_start(out=out_2[0, 4 * q : 4 * q + 4, :].bitcast(I32), in_=out_s[32 * q : 32 * q + 4, :].bitcast(I32))
